import numpy as np, ml_dtypes
CORES = [17,81,89,18,82,90]
N = 6
import mx_ref
NC, G = 128, 4
C = np.float32(2.0 ** -4)
CNT = [[0,32,24,0,72,0],[84,0,12,24,0,8],[24,0,0,64,28,12],[12,4,0,0,28,84],[0,20,64,20,0,24],[8,72,28,20,0,0]]
OFF = [[sum(c[:e]) for e in range(N + 1)] for c in CNT]
BF = ml_dtypes.bfloat16
def cut(t, i, w=512):
    return t[:, w * i:w * i + w]
def tile(rs):
    return np.stack(rs, axis=2).reshape(128, -1).astype(BF)
def layer(w, X):
    out = []
    for i in range(G):
        for t in range(len(X)):
            p = mx_ref.matmul(mx_ref.quantize(cut(w, len(X) * i + t)), X[t])
            z = p if t == 0 else z + p
        out.append(z)
    return out
def gated(Z, g):
    return [(np.maximum(z, 0) * C) * g for z in Z]
def setup_inputs(rng):
    def f(*shape):
        return mx_ref.flush((rng.standard_normal(shape, dtype=np.float32) * np.exp2(rng.integers(-2, 3, shape[:-1] + (1,)))).astype(BF))
    gt = np.broadcast_to((0.125 + 0.875 * rng.random((N, 1, NC))).astype(BF), (N, 128, NC)).copy()
    return {"gt": gt, "x": f(N, 128, 4 * NC), "w1": f(N, 128, G * 512), "w2": f(N, 128, 512)}
def setup_inputs_blocks(rng):
    d = setup_inputs(rng)
    for k in ("x", "w1", "w2"): d[k] = mx_ref.spread(d[k], rng, 4)
    return d
def setup_inputs_wide(rng):
    d = setup_inputs(rng)
    for k in ("x", "w1", "w2"): d[k] = mx_ref.flush((d[k].astype(np.float32) * np.exp2(rng.integers(-8, 9, (N, 1, 1))).astype(np.float32)).astype(BF))
    return d
def setup_inputs_zeros(rng):
    d = setup_inputs(rng); v = d["x"].reshape(N, 128, -1, 4).copy()
    v[np.broadcast_to((rng.random((N, 1, v.shape[2], 1)) < 0.33), v.shape)] = 0
    d["x"] = v.reshape(d["x"].shape)
    return d
def reference(gt, x, w1, w2):
    y = np.zeros((N, 128, NC), np.float32)
    for e in range(N):
        t = np.concatenate([x[j][:, 4 * OFF[j][e]:4 * OFF[j][e + 1]] for j in range(N)], axis=1)
        g = np.concatenate([gt[j][:, OFF[j][e]:OFF[j][e + 1]] for j in range(N)], axis=1).astype(np.float32)
        y[e] = mx_ref.matmul(mx_ref.quantize(w2[e]), mx_ref.quantize(tile(gated(layer(w1[e], [mx_ref.quantize(t)]), g))))
    return {"y": y}

from concourse.bass import DstId, RemoteDMATransfer
from concourse.mybir import dt, AluOpType, ActivationFunctionType

N, NC, SIM = 6, 128, 96
VIA = {
    0: [(2, True)],
    1: [(2, True), (5, False)],
    2: [(0, False), (3, False), (4, True)],
    3: [(1, True), (0, False)],
}
DIRECT = {
    0: [[(4, 0, 72)], [(1, 0, 32)]],
    1: [[(0, 0, 84)], [(3, 0, 24)]],
    2: [[(5, 0, 12)]],
    3: [[(5, 0, 84)], [(4, 0, 28)]],
    4: [[(2, 0, 64)], [(5, 0, 24)], [(3, 0, 20), (1, 0, 20)]],
    5: [[(1, 0, 72)], [(3, 0, 20), (2, 0, 20)], [(0, 0, 8), (2, 20, 8)]],
}

SCRATCH = {
    "gs": ("dram", [128, 2], "bfloat16"),
    "gp": ("dram", [128, 2], "bfloat16"),
    "gl": ("dram", [5, 128, 2], "bfloat16"),
    "gw": ("sbuf", [128, 1280], "bfloat16"),
    "gg": ("sbuf", [128, 128], "bfloat16"),
    "xt": ("sbuf", [128, 512], "bfloat16"),
    "w1t": ("sbuf", [128, 2048], "bfloat16"),
    "w2t": ("sbuf", [128, 512], "bfloat16"),
    "xq": ("sbuf", [128, 128], "float8_e4m3fn_x4"), "xs": ("sbuf", [128, 128], "uint8"),
    "w1q": ("sbuf", [128, 512], "float8_e4m3fn_x4"), "w1s": ("sbuf", [128, 512], "uint8"),
    "w2q": ("sbuf", [128, 128], "float8_e4m3fn_x4"), "w2s": ("sbuf", [128, 128], "uint8"),
    "hq": ("sbuf", [128, 128], "float8_e4m3fn_x4"), "hs": ("sbuf", [128, 128], "uint8"),
    "bq": ("sbuf", [128, 128], "float8_e4m3fn_x4"), "bs": ("sbuf", [128, 128], "uint8"),
    "rq": ("sbuf", [128, 128], "float8_e4m3fn_x4"), "rs": ("sbuf", [128, 128], "uint8"),
    "tt": ("sbuf", [128, 512], "float32"),
    "h": ("sbuf", [128, 512], "bfloat16"),
    "yt": ("sbuf", [128, 128], "float32"),
    "z": ("psum", [128, 2560], "float32"),
}
SEMAPHORES = ["lg", "lx", "l1", "l2", "qx", "q1", "q2", "gd", "gr", "wd", "wr", "gb", "rcod", "rscl", "tok", "sent",
              "m0", "m1", "m2", "m3", "m4", "v0", "v1", "v2", "v3", "hd", "qh", "yc", "st"]


def bits(m):
    return bin(m).count("1")


def lowest(m, k):
    out, i = 0, 0
    while bits(out) < k:
        out |= m & (1 << i)
        i += 1
    return out


def make_plan(T, topo):
    cnt, cores = T.tables["CNT"], T.cores
    off = [[sum(r[:e]) for e in range(N)] for r in cnt]
    pos = [[sum(cnt[i][e] for i in range(j)) for j in range(N)] for e in range(N)]
    jobs = [(topo.may_write(cores[j], cores[e]), j, e, same) for j in sorted(VIA) for e, same in VIA[j]]
    jobs.sort(key=lambda t: t[0])
    used, helper, forced = set(cores), {}, set()
    for free, j, e, same in jobs:
        me = cores[j]
        c = [h for h in range(SIM) if topo.chip(h) == topo.chip(me) and h not in used
             and topo.may_write(h, cores[e]) and (topo.die(h) == topo.die(me)) == same][0]
        used.add(c)
        helper[j, e] = c
        if not free:
            forced.add((j, e))
    slots = []
    for e in range(N):
        src = [j for j in range(N) if cnt[j][e]]
        slots.append([j for j in src if (j, e) not in forced] + [j for j in src if (j, e) in forced])
    plan = {c: [] for c in range(SIM)}
    for j in range(N):
        me, via = cores[j], [e for e, _ in VIA.get(j, [])]
        hops = [helper.get((j, e), cores[e]) for e in range(N) if cnt[j][e]]
        lanes = 0xFFFFFFFF
        for h in hops:
            lanes &= topo.mask(me, h)
        dests, gl = [], lanes
        for e in range(N):
            if cnt[j][e]:
                d = (helper[j, e], None) if (j, e) in forced else (cores[e], slots[e].index(j))
                gl &= topo.mask(me, d[0])
                dests.append(d)
        plan[me].append(("gate", [(lowest(gl, 1), None, dests, "gd")]))
        if via:
            a, b = min(off[j][e] for e in via), max(off[j][e] + cnt[j][e] for e in via)
            to = [(helper[j, e], a) for e in via]
            plan[me].append(("codes", [(lanes, (a, b), [(h, ("r", p)) for h, p in to], "rcod")]))
            plan[me].append(("scales", [(lanes, (a, b), [(h, ("r", p)) for h, p in to], "rscl")]))
        for group in DIRECT[j]:
            trs = []
            for e, o, n in group:
                m = lanes
                if len(group) > 1 and topo.chip(me) == topo.chip(cores[e]):
                    m = lowest(topo.mask(me, cores[e]) & ~lanes, 4)
                a = off[j][e] + o
                trs.append((m, (a, a + n), [(cores[e], ("b", pos[e][j] + o))], "tok"))
            plan[me].append(("codes", trs))
            plan[me].append(("scales", trs))
        for e in via:
            h, a, n = helper[j, e], off[j][e], cnt[j][e]
            m = topo.mask(h, cores[e]) & lanes
            if (j, e) in forced:
                plan[h].append(("gate", [(lowest(m, 1), None, [(cores[e], slots[e].index(j))], "gr")]))
            tr = [(m, (a, a + n), [(cores[e], ("b", pos[e][j]))], "tok")]
            plan[h].append(("codes", tr))
            plan[h].append(("scales", tr))
    got = {c: {} for c in range(SIM)}
    for c in range(SIM):
        for _, trs in plan[c]:
            for m, _, dests, sem in trs:
                for d, _ in dests:
                    got[d][sem] = got[d].get(sem, 0) + bits(m)
    return plan, got, slots, off, pos, cnt


def issue(g, T, topo, what, trs, mine):
    out = []
    for m, cols, dests, sem in trs:
        if what == "gate":
            src = T.gs[:, :] if mine else T.gp[:, :]
            dsts = [T.gp[:, :] if p is None else T.gl[p] for _, p in dests]
        else:
            a, b = cols
            w = b - a
            dsts = []
            if what == "codes":
                src = (T.xq if mine else T.rq)[:, a:b].bitcast(dt.uint8)
                for _, (k, p) in dests:
                    dsts.append((T.bq if k == "b" else T.rq)[:, p:p + w].bitcast(dt.uint8))
            else:
                src = (T.xs if mine else T.rs)[:, a:b]
                for _, (k, p) in dests:
                    dsts.append((T.bs if k == "b" else T.rs)[:, p:p + w])
        ids = []
        for d, _ in dests:
            rid, pid, _ = topo.addr(d)
            ids.append(DstId(rid=rid, pnc=pid))
        out.append(RemoteDMATransfer(dst_ids=ids, dma_engine_mask=m, remote_sem=T.sem[sem], srcs=[src], dsts=dsts))
    g.remote_dma_fused(out, local_sem=T.sem.sent)
    return sum(bits(t[0]) for t in trs)


def rank_program(g, core, T, topo):
    plan, got, slots, off, pos, cnt = make_plan(T, topo)
    S, todo, come = T.sem, plan[core], got[core]
    rank = T.rank_of(core)
    if rank is None:
        if not todo:
            return
        sent = 0
        need = {"gate": "gd", "codes": "rcod", "scales": "rscl"}
        for what, trs in todo:
            g.wait_ge(S[need[what]], come[need[what]])
            sent += issue(g, T, topo, what, trs, False)
        g.wait_ge(S.sent, sent)
        return

    g.scalar.dma_start(T.gs[:, :], T.gt[0:2, :]).then_inc(S.lg, 16)
    g.sync.dma_start(T.xt[:, :], T.x[:, :]).then_inc(S.lx, 16)
    g.sync.dma_start(T.w1t[:, :], T.w1[:, :]).then_inc(S.l1, 16)
    g.sync.dma_start(T.w2t[:, :], T.w2[:, :]).then_inc(S.l2, 16)

    v = g.vector
    v.wait_ge(S.lx, 16)
    v.quantize_mx(T.xq[:, :], T.xs[:, :], T.xt[:, :]).then_inc(S.qx, 1)
    v.wait_ge(S.l1, 16)
    v.quantize_mx(T.w1q[:, :], T.w1s[:, :], T.w1t[:, :]).then_inc(S.q1, 1)
    v.wait_ge(S.l2, 16)
    v.quantize_mx(T.w2q[:, :], T.w2s[:, :], T.w2t[:, :]).then_inc(S.q2, 1)

    sent, ready = 0, False
    g.wait_ge(S.lg, 16)
    for what, trs in todo:
        if what != "gate" and not ready:
            g.wait_ge(S.qx, 1)
            ready = True
        sent += issue(g, T, topo, what, trs, True)

    src = slots[rank]
    kr = come.get("gr", 0)
    kd = come["gd"]
    g.sync.wait_ge(S.gd, kd)
    g.sync.dma_start(T.gw[0:1, 0:256 * kd], T.gl[0:kd]).then_inc(S.wd, 16)
    if kr:
        g.sync.wait_ge(S.gr, kr)
        g.sync.dma_start(T.gw[0:1, 256 * kd:256 * (kd + kr)], T.gl[kd:kd + kr]).then_inc(S.wr, 16)
    for k, j in enumerate(src):
        if k == 0:
            g.wait_ge(S.wd, 16)
        elif k == kd:
            g.wait_ge(S.wr, 16)
        n, p, o = cnt[j][rank], pos[rank][j], 256 * k + off[j][rank]
        g.partition_broadcast(T.gg[:, p:p + n], T.gw[0:1, o:o + n], 128).then_inc(S.gb, 1)
    g.wait_ge(S.sent, sent)

    t = g.tensor
    ms, vs = [S.m0, S.m1, S.m2, S.m3], [S.v0, S.v1, S.v2, S.v3]
    t.wait_ge(S.q1, 1)
    t.wait_ge(S.tok, come["tok"])
    for b in range(4):
        w = slice(128 * b, 128 * b + 128)
        t.matmul_mx(T.z[:, 512 * b:512 * b + 128], T.w1q[:, w], T.w1s[:, w], T.bq[:, :], T.bs[:, :], True, True).then_inc(ms[b], 1)
    v.wait_ge(S.gb, len(src))
    for b in range(4):
        w = slice(128 * b, 128 * b + 128)
        v.wait_ge(ms[b], 1)
        v.tensor_tensor(T.tt[:, w], T.z[:, 512 * b:512 * b + 128], T.gg[:, :], AluOpType.mult).then_inc(vs[b], 1)
        g.scalar.wait_ge(vs[b], 1)
        g.scalar.activation(T.h[:, b:512:4], T.tt[:, w], ActivationFunctionType.Relu, scale=2.0 ** -4).then_inc(S.hd, 1)
    v.wait_ge(S.hd, 4)
    v.quantize_mx(T.hq[:, :], T.hs[:, :], T.h[:, :]).then_inc(S.qh, 1)
    t.wait_ge(S.q2, 1)
    t.wait_ge(S.qh, 1)
    t.matmul_mx(T.z[:, 2048:2176], T.w2q[:, :], T.w2s[:, :], T.hq[:, :], T.hs[:, :], True, True).then_inc(S.m4, 1)
    v.wait_ge(S.m4, 1)
    v.tensor_copy(T.yt[:, :], T.z[:, 2048:2176]).then_inc(S.yc, 1)
    g.sync.wait_ge(S.yc, 1)
    g.sync.dma_start(T.y[:, :], T.yt[:, :]).then_inc(S.st, 16)
    g.sync.wait_ge(S.st, 16)
